import numpy as np, ml_dtypes
CORES = [66,74,82,90,194,202,210,218]
N = 8
BF = ml_dtypes.bfloat16
def gentries(a):
    return np.ascontiguousarray(a.reshape(8, 16, -1).transpose(0, 2, 1)).reshape(8, -1)
def gtable(e):
    e = np.asarray(e); return np.ascontiguousarray(e.reshape(8, -1, 16).transpose(0, 2, 1)).reshape(128, -1).astype(np.int32)
XI, M, E, L, S, RO, D = 2048, 1024, 1024, 1024, 128, 3, 6
LB = 10
def forest(rng):
    o = np.argsort(rng.random((N, 8, M)), axis=-1); k = np.arange(M)
    inner = (2 * k + 2 < M) & (rng.random((N, 8, M)) >= 0.12); sw = rng.integers(0, 2, (N, 8, M))
    k0 = np.zeros_like(o); k1 = np.zeros_like(o)
    np.put_along_axis(k0, o, np.take_along_axis(o, np.where(inner, 2 * k + 1 + sw, k), 2), 2)
    np.put_along_axis(k1, o, np.take_along_axis(o, np.where(inner, 2 * k + 2 - sw, k), 2), 2)
    return o, k0, k1
def begin(rng, o, lo, hi):
    lv = rng.integers(lo, hi, (N, 8, L))
    return np.take_along_axis(o, 2 ** lv - 1 + (rng.random((N, 8, L)) * 2 ** lv).astype(np.int64), 2)
def vals(rng, n):
    return rng.integers(0, 256, (N, 8, 16, n))
def parts(rng):
    o, k0, k1 = forest(rng)
    return dict(o=o, x=vals(rng, XI), prev=rng.integers(0, XI, (N, 8, XI)), z=vals(rng, M), rs=vals(rng, M), kid0=k0, kid1=k1, env=vals(rng, E),
                start=begin(rng, o, LB - 3 - D, LB - 1), cur=rng.integers(0, XI, (N, 8, L)), w=rng.integers(1, 128, (N, 8, 16)), th=rng.integers(1000, 1500, (N, 8, 1)))
def pack(d):
    r = {}
    for k in ("x", "prev", "z", "rs", "kid0", "kid1", "env", "start", "cur", "w", "th"):
        if k in ("x", "z", "rs", "env"): r[k] = np.ascontiguousarray(d[k].reshape(N, 128, -1)).astype(np.float32).astype(BF)
        elif k in ("start", "cur"): r[k] = np.stack([gtable(a) for a in d[k]])
        elif k == "w": r[k] = d[k].reshape(N, 128, 1).astype(np.int32)
        else: r[k] = np.ascontiguousarray(d[k]).astype(np.int32)
    return r
def setup_inputs(rng):
    return pack(parts(rng))
def setup_inputs_full(rng):
    d = parts(rng)
    d["start"][:, ::2, :S] = d["o"][:, ::2, M // 2:M // 2 + S]; d["th"][:, ::2] = 0
    d["start"][::2, :, :S] = d["o"][::2, :, M // 2:M // 2 + S]; d["th"][::2] = 0
    return pack(d)
def setup_inputs_ties(rng):
    d = parts(rng)
    for k in ("x", "z", "rs", "env"): d[k] = d[k] // 64 * 64
    d["th"] = 64 * rng.integers(18, 22, (N, 8, 1))
    return pack(d)
def setup_inputs_alike(rng):
    d = parts(rng); m = np.arange(M)
    d["start"][:, 0] = d["o"][:, 0, M - 1:M]; d["th"][:, 0] = 0
    d["start"][:, 1] = rng.choice(np.array([0, M - 1]), (N, L)); d["cur"][:, 1] = rng.choice(np.array([0, XI - 1]), (N, L))
    d["prev"][:, 1] = np.where(rng.random((N, XI)) < 0.5, np.arange(XI), rng.choice(np.array([0, XI - 1]), (N, XI)))
    d["kid0"][:, 2] = (m + 1) & (M - 1); d["kid1"][:, 2] = (m + 1 + rng.integers(0, M - 1, (N, M))) & (M - 1)
    d["kid0"][:, 3] = m; d["kid1"][:, 3] = m
    d["start"][:, 3] = np.take_along_axis(rng.integers(0, M, (N, 40)), rng.integers(0, 40, (N, L)), 1)
    d["w"][:, 4] = 0; d["th"][:, 4] = 4096
    d["z"][:, 5] = 0; d["rs"][:, 5] = rng.choice(np.array([0, 255]), (N, 16, M))
    d["kid1"][:, 6] = d["kid0"][:, 6]; d["prev"][:, 6] = np.arange(XI)
    d["x"][:, 7] = 255; d["env"][:, 7] = 255; d["w"][:, 7] = 127; d["th"][:, 7] = 0
    return pack(d)
def setup_inputs_edges(rng):
    d = parts(rng); r = np.arange(N)[:, None]
    d["start"][:, :2, :S] = d["o"][:, :2, M // 2:M // 2 + S]; d["env"][:, :2] = 0
    c = rng.integers(0, 256, (16, 1)); d["x"][:, 0] = c
    d["rs"][:, 0] = np.where(rng.random((N, 1, M)) < 0.5, c, d["rs"][:, 0]); d["th"][:, 0] = r & 1
    c = 255 * rng.integers(0, 2, (16, 1)); d["x"][:, 1] = c
    d["rs"][:, 1] = 255 - c; d["rs"][:, 1, 0] = np.abs(255 - c[0] - rng.integers(0, 3, (N, M)))
    d["th"][:, 1] = np.array([4080, 4081, 4096, 4079])[r & 3]
    d["x"][:, 2:4] = rng.integers(250, 256, (N, 2, 16, XI)); d["w"][:, 2:4] = 127; d["env"][:, 3] = 0
    d["th"][:, 3] = rng.integers(2040, 2060, (N, 1))
    d["kid1"][:, 4] = np.where(rng.random((N, M)) < 0.5, d["kid0"][:, 4], d["kid1"][:, 4])
    return pack(d)
def setup_inputs_spread(rng):
    d = parts(rng); m = np.arange(M); lf = rng.random((N, 4, M)) < 0.5
    for k in ("kid0", "kid1"): d[k][:, 1::2] = np.where(lf, m, (m + rng.integers(1, M, (N, 4, M))) & (M - 1))
    for k, n in (("x", XI), ("z", M), ("rs", M), ("env", E)):
        d[k] = np.minimum((np.exp2(8 * rng.random((N, 8, 1, n))) * rng.random((N, 8, 16, n))).astype(np.int64), 255)
    d["w"] = np.minimum(np.exp2(7 * rng.random((N, 8, 16))).astype(np.int64), 127)
    d["th"] = np.minimum(np.exp2(12 * rng.random((N, 8, 1))).astype(np.int64), 4096); d["th"][:, 0] = 1; d["th"][:, 1] = 0
    d["start"] = begin(rng, d["o"], 0, LB)
    d["cur"] = np.minimum((XI * rng.random((N, 8, L)) ** 3).astype(np.int64), XI - 1)
    d["prev"] = np.where(rng.random((N, 8, XI)) < 0.5, np.maximum(np.arange(XI) - rng.integers(0, 40, (N, 8, XI)), 0), d["prev"])
    return pack(d)
def check_inputs(d):
    bad = []
    for k, lo, hi in (("x", 0, 255), ("prev", 0, XI - 1), ("z", 0, 255), ("rs", 0, 255), ("kid0", 0, M - 1), ("kid1", 0, M - 1), ("env", 0, 255), ("start", 0, M - 1), ("cur", 0, XI - 1), ("w", 0, 127), ("th", 0, 4096)):
        a = np.asarray(d[k]).astype(np.float32)
        if not np.all((a >= lo) & (a <= hi) & (a == np.floor(a))): bad.append("range of " + k)
    m = np.arange(M)
    if np.any((np.asarray(d["kid0"]) == m) != (np.asarray(d["kid1"]) == m)): bad.append("one kid of a node is the node itself, the other isn't")
    return bad
def pick(a, ix):
    return np.take_along_axis(a, ix[:, :, None, :], 3)
def reference(x, prev, z, rs, kid0, kid1, env, start, cur, w, th):
    def cols(a, more):
        b = a.astype(np.float32).astype(np.int32).reshape(N, 8, 16, -1)
        return np.concatenate([b, np.zeros((N, 8, 16, more), np.int32)], axis=3)
    X = cols(x, RO * L); Z = cols(z, 2 * S * RO); R = cols(rs, 2 * S * RO); EN = cols(env, 0)
    P = np.concatenate([prev.astype(np.int64), np.zeros((N, 8, RO * L), np.int64)], axis=2)
    own = np.zeros((N, 8, 1), np.int64) + np.arange(M, M + 2 * S * RO)
    K0 = np.concatenate([kid0.astype(np.int64), own], axis=2); K1 = np.concatenate([kid1.astype(np.int64), own], axis=2)
    F0 = np.stack([gentries(a) for a in start]).astype(np.int64); C = np.stack([gentries(a) for a in cur]).astype(np.int64)
    W = w.reshape(N, 8, 16, 1).astype(np.int32); TH = th.reshape(N, 8, 1).astype(np.int64)
    lower = np.arange(S)[None, :] < np.arange(S)[:, None]
    for t in range(RO):
        f = F0; s = C
        for step in range(D):
            k0 = np.take_along_axis(K0, f, 2); k1 = np.take_along_axis(K1, f, 2); go = k0 != f
            b = np.sum(pick(X, s) >= pick(Z, f), axis=2) >= 9
            f = np.where(go, np.where(b, k1, k0), f); s = np.where(go, np.take_along_axis(P, s, 2), s)
        xc = pick(X, C); rf = pick(R, f); a = np.sum(rf > xc, axis=2)
        y = pick(EN, (np.sum(W * xc, axis=2) + 97 * a) & (E - 1)); v = (xc + y) & 255
        fs = f[:, :, :S]; leaf = np.take_along_axis(K0, fs, 2) == fs
        first = ~np.any((fs[:, :, :, None] == fs[:, :, None, :]) & lower, axis=3)
        far = np.sum(np.abs(rf[..., :S] - v[..., :S]), axis=2) >= TH
        q, g, i = np.nonzero(leaf & first & far); at = fs[q, g, i]; n0 = M + 2 * S * t + 2 * i; xs = pick(X, s[:, :, :S])
        Z[q, g, :, at] = xs[q, g, :, i]; K0[q, g, at] = n0; K1[q, g, at] = n0 + 1
        R[q, g, :, n0] = rf[q, g, :, i]; R[q, g, :, n0 + 1] = (rf[q, g, :, i] + v[q, g, :, i]) >> 1
        came = np.roll(v, 1, axis=0)
        h = np.sum(W * came, axis=2) & (L - 1); lo = XI + L * t
        X[..., lo:lo + L] = came; P[..., lo:lo + L] = np.take_along_axis(C, h, 2)
        C = np.zeros((N, 8, 1), np.int64) + np.arange(lo, lo + L)
    return {"yk0": K0.astype(np.float32), "yk1": K1.astype(np.float32), "yr": np.ascontiguousarray(R[..., M:].reshape(N, 128, 2 * S * RO)).astype(np.float32).astype(BF), "yp": np.ascontiguousarray(P[..., XI:]).astype(np.float32)}

from concourse.mybir import AluOpType, AxisListType, ActivationFunctionType
import comms_topo

A = AluOpType
F = ActivationFunctionType
TB = 1920
XAW = 6272
XV = 736
KS = 832

BUFS = {
    "bfloat16": dict(XW=2048, PW=2048, ZW=TB, KW=TB, RW=2048, CT=1792, EM=1024, EP=1024, CP=3072, XA0=XAW, XA1=XAW, BT0=1024,
                     BT1=1024, KG0=1024, KG1=1024, PG0=1024, PG1=1024, SP=1024, TT=1024, PB0=128, PB1=128, KBL=128, KBH=128,
                     KBF=64, KG6=128, CG=128, BE=128, BO=128, EE=64, RN=256, DD=128, DA=128, XV6=128, V4=144, V97=144, VP=144,
                     VKK=144, VK1=144, VW=144, EY=128, G0=240, SCE=128, SCO=128, KN=384, ZB=512, CBB=224),
    "int32": dict(CURI=64, STI=64, PC=128, PCL=128, KC=128, KCL=128, OWN=64, OWN2=64, TM=64, TN=64, FI=64, SWI=64, HI=64, QI=64,
                  QI2=64, OA=256, YI=64, YI2=64, S1=128, V1=128, H1=128, H2=128, IP=1, IQ=3, I14=14, CBI=154,
                  WI=1, THB=8, KI=64, K0=64, K1=64, LF=48, L24=40),
    "uint16": dict(IXP=192, IX=192, SL0=64, SL1=64, ST=64, FL0=64, FL1=64, XL=8, HL=64, OL=64, SCL=8, SCR=16),
    "float32": dict(CURF=64, CURW=1024, YPC=1024, U=64, YF1=64, YF2=64, YK0=112, YK1=112, RJ=1024,
                    FM=8, w8=96, col=64, IC=144, IG=240, ID=128, JN=128, J2=256, I8=8, T0=8, TL=8, T2=8, LN=8, DM=8, THM=8),
}
PSUM = ("pA", "pK", "pP", "pS", "pD0", "pD1", "pM", "pN")
SCRATCH = {n: ("sbuf", [128, w], d) for d, b in BUFS.items() for n, w in b.items()}
SCRATCH["THR"] = ("sbuf", [1, 8], "int32")
SCRATCH["CD"] = ("dram", [16, 1792], "bfloat16")
for _n in PSUM:
    SCRATCH[_n] = ("psum", [128, 512], "float32")
LOADS = ["l_cur", "l_start", "l_prev", "l_kid0", "l_kid1", "l_x", "l_z", "l_env", "l_w", "l_th", "l_rs"]
TAGS = ("e", "c0", "c1", "c2", "i0a", "i0b", "i1a", "i1b", "i2a", "i2b")
SEMAPHORES = ["c_v", "c_s", "c_t", "c_g", "d_p", "d_k", "d_cw", "d_c1", "d_c2", "o_yp0", "o_yp1", "o_yp2", "o_yr0", "o_yr1",
              "o_yk0", "o_yk1"] + LOADS + [a + b for a in ("r_", "q_") for b in TAGS]


def rank_program(g, core, T, topo):
    rank = T.rank_of(core)
    if rank is None:
        return
    nxt = T.cores[(rank + 1) % len(T.cores)]
    prv = T.cores[(rank - 1) % len(T.cores)]
    queues = {"v": g.vector, "s": g.scalar, "t": g.tensor, "y": g.sync, "g": g}
    clock = {q: {} for q in queues}
    total = {}
    hist = {}

    def wait(q, ev):
        sem, val, snap = ev
        c = clock[q]
        if c.get(sem, 0) >= val:
            return
        queues[q].wait_ge(T.sem[sem], val)
        for k, v in snap.items():
            if c.get(k, 0) < v:
                c[k] = v
        c[sem] = val

    def meets(r, s):
        if r[1] >= s[2] or s[1] >= r[2]:
            return False
        return r[3] is None or s[3] is None or r[3] == s[3]

    def spec(r):
        if not isinstance(r, tuple):
            r = (r,)
        r = tuple(r) + (0, 1 << 20, None)[len(r) - 1:]
        return (r[0], 0, 1 << 20, None) if r[0] in PSUM else r

    def need(q, reads, writes):
        own = "c_" + q
        evs = []
        for wr, regs in ((False, reads), (True, writes)):
            for r in regs:
                for s, kind, ev in hist.get(r[0], ()):
                    if meets(r, s) and (ev[0] != own if kind == "p" else (wr or kind == "w")):
                        evs.append(ev)
        evs.sort(key=lambda e: -sum(e[2].values()))
        for ev in evs:
            wait(q, ev)

    def note(ev, reads, writes):
        for wr, regs in ((False, reads), (True, writes)):
            for r in regs:
                h = hist.setdefault(r[0], [])
                p = r[0] in PSUM
                if wr and not p:
                    h[:] = [e for e in h if not (r[3] is None and r[1] <= e[0][1] and e[0][2] <= r[2])]
                else:
                    kd = "p" if p else "r"
                    h[:] = [e for e in h if not (e[1] == kd and e[0] == r and e[2][0] == ev[0] and e[2][1] <= ev[1])]
                h.append((r, "p" if p else ("w" if wr else "r"), ev))

    def op(q, fn, reads, writes, sem=None, inc=1, group=None):
        reads = [spec(r) for r in reads]
        writes = [spec(r) for r in writes]
        need(q, reads, writes)
        ins = fn()
        sem = sem or "c_" + q
        ins.then_inc(T.sem[sem], inc)
        total[sem] = total.get(sem, 0) + inc
        note((sem, group or total[sem], dict(clock[q])), reads, writes)

    def dma(q, sem, out, in_, reads, writes, n=1):
        op(q, lambda: queues[q].dma_start(out, in_), reads, writes, sem=sem, inc=16, group=16 * n)

    def ts(out, w, in0, r, s1, s2, op0, op1=None):
        def fn():
            if op1 is None:
                return g.vector.tensor_scalar(out, in0, s1, None, op0)
            return g.vector.tensor_scalar(out, in0, s1, s2, op0, op1)
        op("v", fn, r, w)

    def tt(out, w, in0, in1, r, o):
        op("v", lambda: g.vector.tensor_tensor(out, in0, in1, o), r, w)

    def cp(out, w, in_, r):
        op("v", lambda: g.vector.tensor_copy(out, in_), r, w)

    def fill(name, lo, hi, c):
        op("v", lambda: g.vector.memset(T[name][:, lo:hi], c), [], [(name, lo, hi)])

    def act(out, w, in_, r, func=F.Copy, **kw):
        op("s", lambda: g.scalar.activation(out, in_, func, **kw), r, w)

    def iota(name, pattern, base, cm, small):
        if small:
            op("g", lambda: g.iota(T[name][:], pattern, base, cm, allow_small_or_imprecise_dtypes=True), [], [name])
        else:
            op("g", lambda: g.iota(T[name][:], pattern, base, cm), [], [name])

    def wrap(ps, lt, src, base, n, start=True, stop=True, contiguous=False):
        m = n // 16

        def fn():
            r = None
            for k in range(16):
                if contiguous:
                    rhs = T[src][:, base + k * m:base + (k + 1) * m]
                else:
                    rhs = T[src][:, base + k:base + n:16]
                r = g.tensor.matmul(T[ps][:, 0:m], T[lt][:, 15 - k:143 - k], rhs, start and k == 0, stop and k == 15)
            return r
        op("t", fn, [lt, (src, base, base + n)], [ps])

    def send(tag, dst, dlo, src, lo, hi):
        need("g", [spec((src, lo, hi))], [])
        rid, pid = topo.addr(nxt, core)
        g.remote_dma(T[dst][:, dlo:dlo + hi - lo], T[src][:, lo:hi], T.sem["r_" + tag], T.sem["q_" + tag], pid, rid,
                     topo.mask(core, nxt))
        n = len(topo.engines(core, nxt))
        total["q_" + tag] = n
        note(("q_" + tag, n, dict(clock["g"])), [spec((src, lo, hi))], [])
        m = len(topo.engines(prv, core))
        total["r_" + tag] = m
        note(("r_" + tag, m, {}), [], [spec((dst, dlo, dlo + hi - lo))])

    def gx(q, dst, d0, src, s0, s1, lst, lo, hi):
        if lo >= hi:
            return
        out, w = T[dst][:, d0 + lo:d0 + hi], [(dst, d0 + lo, d0 + hi)]
        in_, r = T[src][:, s0:s1].indirect(T[lst][:, lo // 16:hi // 16]), [(src, s0, s1), (lst, lo // 16, hi // 16)]
        if q == "v":
            cp(out, w, in_, r)
        else:
            act(out, w, in_, r)

    ncol = [0]

    def col():
        ncol[0] += 1
        return T.col[:, ncol[0] - 1:ncol[0]], ("col", ncol[0] - 1, ncol[0])

    def colop(a, s1, s2, op0, op1=None):
        c, w = col()
        ts(c, [w], a[0], [a[1]], s1, s2, op0, op1)
        return c, w

    def colsum(a, b, o=A.add):
        c, w = col()
        tt(c, [w], a[0], b[0], [a[1], b[1]], o)
        return c, w

    dma("y", "l_cur", T.CURI[:], T.cur[:, :], [], ["CURI"])
    dma("s", "l_kid0", T.KC[:, 0:64], T.kid0[:, :], [], [("KC", 0, 64)])
    dma("y", "l_prev", T.PC[:], T.prev[:, :], [], ["PC"])
    dma("s", "l_kid1", T.KC[:, 64:128], T.kid1[:, :], [], [("KC", 64, 128)])
    dma("s", "l_start", T.STI[:], T.start[:, :], [], ["STI"])
    dma("y", "l_x", T.XW[:], T.x[:, :], [], ["XW"])

    iota("IP", [[0, 1]], 0, 1, False)
    iota("IC", [[1, 144]], -15, 0, True)
    iota("OWN", [[1, 64]], 0, 64, False)
    iota("I14", [[1, 14]], 0, 14, False)
    iota("I8", [[1, 8]], 0, 0, True)
    iota("T0", [[16, 8]], 1792, 0, True)
    iota("J2", [[1, 256]], 0, 0, True)
    iota("JN", [[-1, 128]], -1, 0, True)
    iota("ID", [[1, 128]], 0, -1, True)
    iota("IG", [[1, 240]], -112, 0, True)
    iota("CURW", [[1, 1024]], 0, 0, True)

    fill("ZB", 0, 512, 0.0)
    for b, lo, hi in (("KW", 0, 512), ("KW", 512, 1024), ("KW", 1024, 1536), ("KW", 1536, TB), ("ZW", 1024, 1536),
                      ("ZW", 1536, TB), ("RW", 1024, 1536), ("RW", 1536, 2048)):
        act(T[b][:, lo:hi], [(b, lo, hi)], T.ZB[:, 0:hi - lo], ["ZB"])
    fill("PW", 0, 2048, 0.0)
    ip = (T.IP[:], ("IP", 0, 1))
    for i, (n, o) in enumerate(((4, A.arith_shift_right), (15, A.bitwise_and), (31, A.bitwise_and))):
        ts(T.IQ[:, i:i + 1], [("IQ", i, i + 1)], T.IP[:], ["IP"], n, None, o)
    ts(T.OWN2[:], ["OWN2"], T.OWN[:], ["OWN"], 1023, None, A.bitwise_and)
    iq = [(T.IQ[:, i:i + 1], ("IQ", i, i + 1)) for i in range(3)]
    p4, p16 = colop(iq[0], 1.0, None, A.mult), colop(iq[0], 16.0, None, A.mult)
    p15, p31 = colop(iq[1], 1.0, None, A.mult), colop(iq[2], 1.0, None, A.mult)

    cp(T.SL0[:], ["SL0"], T.CURI[:], ["CURI"])
    ts(T.PCL[:], ["PCL"], T.PC[:], ["PC"], 255, None, A.bitwise_and)
    cp(T.PB0[:], ["PB0"], T.PCL[:], ["PCL"])
    tt(T.PB1[:], ["PB1"], T.PC[:], T.PCL[:], ["PC", "PCL"], A.subtract)
    dma("y", "d_p", T.PW[0:128:16, :], T.PB0[:], ["PB0"], [("PW", 0, 2048, 0)], 2)
    dma("y", "d_p", T.PW[1:128:16, :], T.PB1[:], ["PB1"], [("PW", 0, 2048, 1)], 2)
    ts(T.KCL[:], ["KCL"], T.KC[:], ["KC"], 255, None, A.bitwise_and)
    tt(T.KBF[:], ["KBF"], T.KC[:, 0:64], T.OWN2[:], [("KC", 0, 64), "OWN2"], A.is_equal)
    cp(T.KBL[:], ["KBL"], T.KCL[:], ["KCL"])
    tt(T.KBH[:], ["KBH"], T.KC[:], T.KCL[:], ["KC", "KCL"], A.subtract)
    for q, b, lo in ((15, "KBF", 0), (0, "KBL", 0), (2, "KBL", 64), (1, "KBH", 0), (3, "KBH", 64)):
        dma("y", "d_k", T.KW[q:128:16, 0:1024], T[b][:, lo:lo + 64], [(b, lo, lo + 64)], [("KW", 0, 1024, q)], 5)
    dma("y", "l_z", T.ZW[:, 0:1024], T.z[:, :], [], [("ZW", 0, 1024)])
    dma("y", "l_w", T.WI[:], T.w[:, :], [], ["WI"])
    dma("y", "l_th", T.THR[:], T.th[:, :], [], ["THR"])
    dma("y", "l_env", T.EM[:], T.env[:, :], [], ["EM"])
    dma("y", "l_rs", T.RW[:, 0:1024], T.rs[:, :], [], [("RW", 0, 1024)])

    def vmat(name, s2, more=()):
        ts(T[name][:], [name], T.IC[:], ["IC", p16[1]] + list(more), p16[0], s2, A.is_equal, A.mult)

    wp, lt4 = colop(p15, 2.0, None, A.is_lt), colop(p15, 4.0, None, A.is_lt)
    eq15 = colop(p15, 15.0, None, A.is_equal)
    m15 = colop(eq15, 4194304.0, None, A.mult)
    wk1 = colsum(lt4, wp, A.subtract)
    ws = colsum(wp, m15)
    wk2 = colop(wk1, 2048.0, None, A.mult)
    cp(T.ST[:], ["ST"], T.STI[:], ["STI"])
    vmat("VP", wp[0], [wp[1]])
    vmat("V4", 4096.0)
    wkk = colsum(ws, wk2)
    vmat("VK1", wk1[0], [wk1[1]])
    vmat("VKK", wkk[0], [wkk[1]])

    def more_columns():
        re, ro = colop(p31, 15.0, None, A.is_equal), colop(p31, 31.0, None, A.is_equal)
        ce, c27 = colop(p31, 11.0, 64.0, A.is_lt, A.mult), colop(p31, 27.0, 64.0, A.is_lt, A.mult)
        c16 = colop(p31, 16.0, 64.0, A.is_lt, A.mult)
        rb = colop(ip, -703.0, None, A.add)
        e0, e1 = colop(p15, 0.0, None, A.is_equal), colop(p15, 1.0, None, A.is_equal)
        e2, e3 = colop(p15, 2.0, None, A.is_equal), colop(p15, 3.0, None, A.is_equal)
        co, c13, c02 = colsum(c27, c16, A.subtract), colsum(e1, e3), colsum(e0, e2)
        c02d = colop(c02, 2.0, None, A.mult)
        his = [colop(c13, 1024.0 + 256 * t, None, A.mult) for t in range(3)]
        return re, ro, ce, co, rb, c02, c02d, [colsum(h, e2) for h in his], [colsum(h, eq15) for h in his]

    def scaled(out, w, in_, r, s, b):
        act(out, [w], in_, [r, s[1], b[1]], F.Identity, scale=s[0], bias=b[0])

    def tables():
        scaled(T.SCE[:], "SCE", T.JN[:], "JN", re, ce)
        scaled(T.SCO[:], "SCO", T.JN[:], "JN", ro, co)
        for t in range(3):
            lo, hi = 128 * t, 1024 + 256 * t
            scaled(T.KN[:, lo:lo + 128], ("KN", lo, lo + 128), T.J2[:, 0:128], "J2", c02d, kbs[t])
            scaled(T.KW[:, hi:hi + 256], ("KW", hi, hi + 256), T.J2[:], "J2", c02, kcs[t])

    def hand_ahead():
        wf = colop((T.WI[:], "WI"), 1.0, None, A.mult)
        vmat("VW", wf[0], [wf[1]])
        ts(T.EM[:], ["EM"], T.EM[:], ["EM"], -256.0, None, A.add)
        send("c0", "CP", 0, "XA0", 0, 1024)
        send("e", "EP", 0, "EM", 0, 1024)

    def codes():
        for b in range(11):
            ts(T.CBI[:, 14 * b:14 * b + 14], [("CBI", 14 * b, 14 * b + 14)], T.I14[:], ["I14"], b, 1, A.arith_shift_right,
               A.bitwise_and)
        fill("CBB", 154, 210, 0.0)
        fill("CBB", 210, 224, 1.0)
        ts(T.CBB[:, 0:154], [("CBB", 0, 154)], T.CBI[:], ["CBI"], 2.0, -1.0, A.mult, A.add)
        for q in range(16):
            dma("y", "d_c1", T.CD[q, :], T.CBB[:, 14 * q:14 * q + 14], [("CBB", 14 * q, 14 * q + 14)], [("CD", 0, 1792, q)], 16)
        for q in range(8):
            dma("y", "d_c2", T.CT[16 * q:16 * q + 16, :], T.CD[:, :], ["CD"], [("CT", 0, 1792, q)], 8)
        cp(T.CURF[:], ["CURF"], T.CURI[:], ["CURI"])
        dma("y", "d_cw", T.CURW[0:128:16, :], T.CURF[:], ["CURF"], ["CURW"])

    def thresholds():
        vmat("V97", 97.0)
        ts(T.DM[:], ["DM"], T.I8[:], ["I8", p4[1]], p4[0], None, A.is_equal)
        op("g", lambda: g.partition_broadcast(T.THB[:], T.THR[:], 128), ["THR"], ["THB"])
        ts(T.TL[:], ["TL"], T.T0[:], ["T0", p15[1]], p15[0], None, A.add)
        ts(T.EY[:], ["EY"], T.ID[:], ["ID"], 0.0, None, A.is_equal)
        ts(T.G0[:], ["G0"], T.IG[:], ["IG", p15[1]], p15[0], None, A.is_equal)
        tt(T.THM[:], ["THM"], T.THB[:], T.DM[:], ["THB", "DM"], A.mult)
        ts(T.T2[:], ["T2"], T.TL[:], ["TL"], 2.0, -1792.0, A.mult, A.add)
        ts(T.LN[:], ["LN"], T.TL[:], ["TL"], 4352.0, None, A.add)
        c, w = col()
        op("v", lambda: g.vector.tensor_reduce(c, T.THM[:], AxisListType.X, A.add), ["THM"], [w])
        return colop((c, w), 4096.0, None, A.mult)

    def zcmp(t, k):
        xa, lst, b = "XA%d" % (t % 2), "FL%d" % (k % 2) if k else "ST", "BT%d" % (k % 2)
        lo, hi = 1024 * k, 1024 * k + 1024
        tt(T[b][:], [b], T.ZW[:].indirect(T[lst][:]), T[xa][:, lo:hi], ["ZW", lst, (xa, lo, hi)], A.is_le)

    def kgather(k, ks=1024):
        for q, lo, hi in (("s", 0, ks), ("v", ks, 1024)):
            gx(q, "KG%d" % (k % 2), 0, "KW", 0, TB, "FL%d" % (k % 2) if k else "ST", lo, hi)

    def wraps(k):
        wrap("pK", "VKK", "KG%d" % (k % 2), 0, 1024)
        wrap("pA", "V4", "BT%d" % (k % 2), 0, 1024)

    def select(k):
        fl = "FL%d" % ((k + 1) % 2)
        cp(T.KI[:], ["KI"], T.pK[:, 0:64], ["pK"])
        ts(T.K0[:], ["K0"], T.KI[:], ["KI"], 2047, None, A.bitwise_and)
        ts(T.K1[:], ["K1"], T.KI[:], ["KI"], 11, 2047, A.arith_shift_right, A.bitwise_and)
        ts(T.U[:], ["U"], T.K0[:], ["K0"], 34816.0, None, A.add)
        ts(T.LF[:, 8 * k:8 * k + 8], [("LF", 8 * k, 8 * k + 8)], T.KI[:, 0:8], ["KI"], 12, 1024, A.arith_shift_right, A.bitwise_and)
        tt(T.TN[:], ["TN"], T.pA[:, 0:64], T.K1[:], ["pA", "K1"], A.add)
        tt(T.TM[:], ["TM"], T.TN[:], T.U[:], ["TN", "U"], A.max)
        ts(T.FI[:], ["FI"], T.TM[:], ["TM"], 2047, None, A.bitwise_and)
        cp(T[fl][:], [fl], T.FI[:], ["FI"])

    th = None
    gx("v", "XA0", 0, "XW", 0, 2048, "SL0", 0, 1024)
    for k in range(6):
        sl, sn, pg = "SL%d" % (k % 2), "SL%d" % ((k + 1) % 2), "PG%d" % (k % 2)
        n = 1024 if k < 5 else 128
        gx("s", pg, 0, "PW", 0, 2048, sl, 0, n)
        if k:
            gx("s", "XA0", 1024 * k, "XW", 0, 2048, sl, XV, 1024)
        if k == 5:
            tables()
        kgather(k)
        zcmp(0, k)
        if k == 0:
            re, ro, ce, co, rb, c02, c02d, kbs, kcs = more_columns()
        wrap("pP", "VP", pg, 0, n)
        wraps(k)
        cp(T[sn][:, 0:n // 16], [(sn, 0, n // 16)], T.pP[:, 0:n // 16], ["pP"])
        if k < 5:
            gx("v", "XA0", 1024 * k + 1024, "XW", 0, 2048, sn, 0, XV)
        else:
            gx("s", "XA0", 6144, "XW", 0, 2048, sn, 0, 128)
            th = thresholds()
        if k == 0:
            hand_ahead()
        if k == 1:
            wrap("pS", "VW", "XA0", 0, 1024)
            codes()
        if k == 2:
            cp(T.SWI[:], ["SWI"], T.pS[:, 0:64], ["pS"])
        select(k)

    def end_of_round(t):
        xa, x0, fl = "XA%d" % (t % 2), 64 * t, "FL0"
        gx("s", "CG", 0, "CT", 0, 1792, fl, 0, 128)
        gx("s", "RN", 0, "RW", 0, 2048, fl, 0, 128)
        gx("s", "KG6", 0, "KW", 0, TB, fl, 0, 128)
        for h in range(2):
            lo, hi = 512 * h, 512 * h + 512
            tt(T.BT0[:, lo:hi], [("BT0", lo, hi)], T.RW[:].indirect(T[fl][:, lo // 16:hi // 16]), T[xa][:, lo:hi],
               ["RW", (fl, lo // 16, hi // 16), (xa, lo, hi)], A.is_gt)
            wrap("pS" if h else "pP", "V97", "BT0", lo, 512)

        def column(h):
            q0, q1, ps = 32 * h, 32 * h + 32, "pS" if h else "pP"
            tt(T.QI[:, q0:q1], [("QI", q0, q1)], T[ps][:, 0:32], T.SWI[:, q0:q1], [ps, "SWI"], A.add)
            ts(T.QI2[:, q0:q1], [("QI2", q0, q1)], T.QI[:, q0:q1], [("QI", q0, q1)], 1023, None, A.bitwise_and)
            cp(T.IX[:, x0 + q0:x0 + q1], [("IX", x0 + q0, x0 + q1)], T.QI2[:, q0:q1], [("QI2", q0, q1)])
            send("i%d" % t + "ab"[h], "IXP", x0 + q0, "IX", x0 + q0, x0 + q1)
        column(0)
        tt(T.BE[:], ["BE"], T.CG[:], T.SCE[:], ["CG", "SCE"], A.mult)
        tt(T.BO[:], ["BO"], T.CG[:], T.SCO[:], ["CG", "SCO"], A.mult)
        column(1)
        banks = ("pD0", "pD1", "pK", "pN")

        def dots(a):
            def fn():
                r = None
                for i, b in enumerate((T.BE, T.BO)):
                    r = g.tensor.matmul(T[banks[a]][:, 128 * i:128 * i + 128], T.CG[32 * a:32 * a + 32, :],
                                        b[32 * a:32 * a + 32, :], True, True)
                return r
            op("t", fn, ["CG", "BE", "BO"], [banks[a]])
        for a in range(4):
            dots(a)
        wrap("pA", "VKK", "KG6", 0, 128)
        for q in range(8):
            ps, i = banks[q // 2], 128 * (q % 2)

            def relu(q=q, ps=ps, i=i):
                return g.scalar.activation(T.RJ[:, 128 * q:128 * q + 128], T[ps][:, i:i + 128], F.Relu, bias=rb[0],
                                           accum_out=T.FM[:, q:q + 1])
            op("s", relu, [ps, rb[1]], [("RJ", 128 * q, 128 * q + 128), ("FM", q, q + 1)])
        tt(T.S1[:], ["S1"], T.EM[:].indirect(T.IX[:, x0:x0 + 8]), T[xa][:, 0:128], ["EM", ("IX", x0, x0 + 8), (xa, 0, 128)], A.add)
        ts(T.V1[:], ["V1"], T.S1[:], ["S1"], 255, None, A.bitwise_and)
        tt(T.DD[:], ["DD"], T.RN[:, 0:128], T.V1[:], [("RN", 0, 128), "V1"], A.subtract)
        act(T.DA[:], ["DA"], T.DD[:], ["DD"], F.Abs)
        if t < 2:
            l = [(T.L24[:, 8 * i:8 * i + 8], ("L24", 8 * i, 8 * i + 8)) for i in range(5)]
            tt(T.L24[:, 0:24], [("L24", 0, 24)], T.LF[:, 0:24], T.LF[:, 24:48], ["LF"], A.add)
            tt(l[3][0], [l[3][1]], l[0][0], l[1][0], [l[0][1], l[1][1]], A.add)
            tt(l[4][0], [l[4][1]], T.LN[:], l[2][0], [l[2][1], "LN"], A.subtract)
            tt(l[0][0], [l[0][1]], l[4][0], l[3][0], [l[3][1], l[4][1]], A.subtract)
            cp(T.XL[:], ["XL"], l[0][0], [l[0][1]])
            gx("s", "XV6", 0, xa, 0, XAW, "XL", 0, 128)
        lf, ft, fi, fq, fa, sa, sb, ra, rd = [(T.w8[:, 8 * i:8 * i + 8], ("w8", 8 * i, 8 * i + 8)) for i in range(9)]
        ts(lf[0], [lf[1]], T.pA[:, 0:8], ["pA"], 4194304.0, None, A.is_ge)
        tt(ft[0], [ft[1]], T.FI[:, 0:8], T.TL[:], [("FI", 0, 8), "TL"], A.subtract)
        for q in range(8):
            ts(T.EE[:, 8 * q:8 * q + 8], [("EE", 8 * q, 8 * q + 8)], T.DM[:], ["DM", ("FM", q, q + 1)], T.FM[:, q:q + 1], None,
               A.is_gt)

        def conv():
            r = None
            for q in range(8):
                r = g.tensor.matmul(T.pP[:, 0:8], T.G0[:, 112 - 16 * q:240 - 16 * q], T.EE[:, 8 * q:8 * q + 8], q == 0, q == 7)
            return r
        wrap("pM", "V4", "DA", 0, 128)
        op("t", conv, ["G0", "EE"], ["pP"])

        def split_lists():
            ts(fa[0], [fa[1]], T.pM[:, 0:8], ["pM", th[1]], th[0], None, A.is_ge)
            tt(fi[0], [fi[1]], T.pP[:, 0:8], lf[0], ["pP", lf[1]], A.mult)
            tt(sa[0], [sa[1]], fi[0], fa[0], [fi[1], fa[1]], A.mult)
            tt(fq[0], [fq[1]], sa[0], ft[0], [sa[1], ft[1]], A.mult)
            tt(sb[0], [sb[1]], fq[0], T.TL[:], [fq[1], "TL"], A.add)
            cp(T.SCL[:], ["SCL"], sb[0], [sb[1]])
            lo, hi = 128 * t, 128 * t + 128
            cp(T.KW[:].indirect(T.SCL[:]), ["KW"], T.KN[:, lo:hi], [("KN", lo, hi), "SCL"])

        def split_z():
            cp(T.ZW[:].indirect(T.SCL[:]), ["ZW"], T.XV6[:], ["XV6", "SCL"])

        def new_r():
            ts(ra[0], [ra[1]], sa[0], [sa[1]], 256.0 * t - 768.0, None, A.mult)
            tt(T.H1[:], ["H1"], T.RN[:, 0:128], T.V1[:], [("RN", 0, 128), "V1"], A.add)
            tt(rd[0], [rd[1]], ra[0], T.T2[:], [ra[1], "T2"], A.add)
            ts(T.H2[:], ["H2"], T.H1[:], ["H1"], 1, None, A.arith_shift_right)
            cp(T.SCR[:, 0:8], [("SCR", 0, 8)], rd[0], [rd[1]])
            ts(T.SCR[:, 8:16], [("SCR", 8, 16)], rd[0], [rd[1]], 1.0, None, A.add)
            cp(T.RN[:, 128:256], [("RN", 128, 256)], T.H2[:], ["H2"])

        def split_r():
            cp(T.RW[:].indirect(T.SCR[:]), ["RW"], T.RN[:], ["RN", "SCR"])
            if t == 1:
                dma("y", "o_yr0", T.yr[:, 0:512], T.RW[:, 1024:1536], [("RW", 1024, 1536)], [])
            if t == 2:
                dma("y", "o_yr1", T.yr[:, 512:768], T.RW[:, 1536:1792], [("RW", 1536, 1792)], [])
        return split_lists, split_z, new_r, split_r

    def arrive(t, h):
        lo, hi, x0, c0 = 512 * h, 512 * h + 512, 64 * t, 1024 * t
        tt(T.SP[:, lo:hi], [("SP", lo, hi)], T.EP[:].indirect(T.IXP[:, x0 + lo // 16:x0 + hi // 16]), T.CP[:, c0 + lo:c0 + hi],
           ["EP", ("IXP", x0 + lo // 16, x0 + hi // 16), ("CP", c0, c0 + 1024)], A.add)
        ts(T.TT[:, lo:hi], [("TT", lo, hi)], T.SP[:, lo:hi], [("SP", lo, hi)], 0.0, 256.0, A.is_lt, A.mult)

    def preds():
        wrap("pN", "VW", "SP", 0, 1024, True, False, True)
        wrap("pN", "VW", "TT", 0, 1024, False, True, True)

    def preds_out(t):
        yf = "YF%d" % t
        cp(T.YI[:], ["YI"], T.pN[:, 0:64], ["pN"])
        ts(T.YI2[:], ["YI2"], T.YI[:], ["YI"], 1023, None, A.bitwise_and)
        ts(T[yf][:], [yf], T.YI2[:], ["YI2"], 1024.0 + 1024 * t, None, A.add)
        dma("y", "o_yp%d" % t, T.yp[:, 1024 * t:1024 * t + 1024], T[yf][:], [yf], [])

    late = end_of_round(0)
    for t in (1, 2):
        xo, xa = "XA%d" % ((t - 1) % 2), "XA%d" % (t % 2)
        for h in range(2):
            lo, hi, pd = 512 * h, 512 * h + 512, "pD%d" % h
            arrive(t - 1, h)

            def vsum(pd=pd, lo=lo, hi=hi):
                g.tensor.matmul(T[pd][:], T.EY[:], T.SP[:, lo:hi], True, False)
                return g.tensor.matmul(T[pd][:], T.EY[:], T.TT[:, lo:hi], False, True)
            op("t", vsum, ["EY", ("SP", lo, hi), ("TT", lo, hi)], [pd])
            act(T[xa][:, lo:hi], [(xa, lo, hi)], T[pd][:], [pd])
            if h == 0:
                late[0]()
                kgather(0)
        late[1]()
        wrap("pS", "VW", "SP", 0, 1024, True, False)
        wrap("pS", "VW", "TT", 0, 1024, False, True)
        send("c%d" % t, "CP", 1024 * t, xa, 0, 1024)
        zcmp(t, 0)
        cp(T.SWI[:], ["SWI"], T.pS[:, 0:64], ["pS"])
        ts(T.HI[:], ["HI"], T.SWI[:], ["SWI"], 1023, None, A.bitwise_and)
        cp(T.HL[:], ["HL"], T.HI[:], ["HI"])
        for k in range(6):
            if k:
                kgather(k, KS)
                zcmp(t, k)
            wraps(k)
            d0 = 1024 * k
            if k < 5:
                gx("s", xa, d0 + 1024, xo, d0, d0 + 1024, "HL", 0, 1024)
            elif t < 2:
                gx("s", xa, d0 + 1024, xo, d0, d0 + 1024, "HL", 0, 128)
            if k == 1:
                late[2]()
            if k == 2:
                late[3]()
            if k == 3 and t == 2:
                preds()
            if k == 4 and t == 2:
                preds_out(1)
            if k == 3 and t == 1:
                oa, ob, oc, od = [(T.OA[:, 64 * i:64 * i + 64], ("OA", 64 * i, 64 * i + 64)) for i in range(4)]
                ts(oa[0], [oa[1]], T.HI[:], ["HI"], 15, None, A.bitwise_and)
                ts(ob[0], [ob[1]], T.HI[:], ["HI"], 4, None, A.arith_shift_right)
                ts(oc[0], [oc[1]], oa[0], [oa[1]], 64.0, None, A.mult)
                tt(od[0], [od[1]], oc[0], ob[0], [oc[1], ob[1]], A.add)
                cp(T.OL[:], ["OL"], od[0], [od[1]])
            select(k)
        late = end_of_round(t)
        if t == 1:
            gx("s", "YPC", 0, "CURW", 0, 1024, "OL", 0, 1024)
            dma("y", "o_yp0", T.yp[:, 0:1024], T.YPC[0:128:16, :], ["YPC"], [])

    arrive(2, 0)
    late[0]()
    wrap("pK", "VP", "KW", 0, 1792, contiguous=True)
    wrap("pA", "VK1", "KW", 0, 1792, contiguous=True)
    act(T.YK0[:], ["YK0"], T.pK[:, 0:112], ["pK"])
    act(T.YK1[:], ["YK1"], T.pA[:, 0:112], ["pA"])
    dma("y", "o_yk0", T.yk0[:, :], T.YK0[:], ["YK0"], [])
    dma("y", "o_yk1", T.yk1[:, :], T.YK1[:], ["YK1"], [])
    arrive(2, 1)
    preds()
    late[2]()
    late[3]()
    preds_out(2)
    for sem in sorted(total):
        wait("g", (sem, total[sem], {}))
